import numpy as np
import ml_dtypes


def mxq(x, axis, fmt="e4m3"):
    dtype, down = {"e4m3": (ml_dtypes.float8_e4m3fn, 7), "e5m2": (ml_dtypes.float8_e5m2, 14)}[fmt]
    v = np.moveaxis(np.asarray(x, np.float32).astype(ml_dtypes.bfloat16).astype(np.float64), axis, -1)
    blocks = v.reshape(v.shape[:-1] + (-1, 32))
    amax = np.abs(blocks).max(-1, keepdims=True)
    byte = np.maximum(np.where(amax > 0, np.frexp(amax)[1] - 1 + 127, 0) - down, 1)
    scale = np.exp2(byte - 127.0)
    codes = (blocks / scale).astype(np.float32).astype(dtype).astype(np.float64)
    return np.moveaxis((codes * scale).reshape(v.shape), -1, axis)


WIDE = False


def mx_kscale(k):
    if not WIDE:
        return np.ones(k)
    levels = np.array([10, -10, 5, -5, 0])
    if k % 512:
        return np.exp2(np.random.permutation(np.resize(levels, k // 32))).repeat(32)
    a = np.empty((k // 512, 16))
    for p in range(k // 512):
        a[p, :8] = np.random.permutation(np.resize(levels, 8))
        for g in range(8):
            far = levels[np.abs(levels - a[p, g]) >= 10]
            a[p, g + 8] = far[np.random.randint(len(far))]
    return np.exp2(a.ravel()).repeat(32)


def f64(x):
    return np.asarray(x).astype(np.float64)


def striped(idx):
    return np.tile(idx.reshape(-1, 16).T, (8, 1)).astype(np.uint16)


def unstriped(offs):
    return offs[:16].T.reshape(-1).astype(np.int64)


E2M1 = np.array([0.0, 0.5, 1.0, 1.5, 2.0, 3.0, 4.0, 6.0, -0.0, -0.5, -1.0, -1.5, -2.0, -3.0, -4.0, -6.0])


def pack_weight(w, fmt):
    k, n = w.shape
    w = f64(np.asarray(w, np.float32).astype(ml_dtypes.bfloat16)).reshape(k // 32, 32, n)
    amax = np.abs(w).max(1)
    if fmt == "e4m3":
        byte = np.frexp(amax)[1] - 1 + 127 - 7
    else:
        mant, ex = np.frexp(amax / 6.0)
        byte = np.where(mant > 0.5, ex, ex - 1) + 127
    byte = np.clip(np.where(amax > 0, byte, 1), 1, 254)
    scaled = (w * np.exp2(127.0 - byte)[:, None, :]).reshape(k, n).astype(np.float32)
    by_word = np.ascontiguousarray(scaled.reshape(k // 512, 128, 4, n).transpose(0, 1, 3, 2))
    if fmt == "e4m3":
        words = by_word.astype(ml_dtypes.float8_e4m3fn).view(np.uint8)
    else:
        c = by_word.astype(ml_dtypes.float4_e2m1fn).view(np.uint8) & 0xF
        words = (c[..., 0::2] | (c[..., 1::2] << 4)).reshape(k // 512, 128, 2 * n)
    return np.ascontiguousarray(words), np.ascontiguousarray(byte.astype(np.uint8).reshape(k // 512, 16, n))


def unpack_weight(words, scales, fmt):
    g, _, n = scales.shape
    words = np.ascontiguousarray(words).reshape(g, 128, n, -1)
    if fmt == "e4m3":
        vals = words.view(ml_dtypes.float8_e4m3fn).astype(np.float64)
    else:
        nib = np.empty((g, 128, n, 4), np.uint8)
        nib[..., 0::2] = words & 0xF
        nib[..., 1::2] = words >> 4
        vals = E2M1[nib]
    vals = vals * np.repeat(np.exp2(scales.astype(np.float64) - 127.0), 8, axis=1)[..., None]
    return vals.transpose(0, 1, 3, 2).reshape(g * 512, n)


def gelu(v):
    return 0.5 * v * (1.0 + np.tanh(np.sqrt(2.0 / np.pi) * (v + 0.044715 * v**3)))


K, H, T, S, P = 1024, 1024, 4096, 1024, 512


def setup_inputs():
    n = np.random.standard_normal
    s = mx_kscale(K)[:, None]
    u = mx_kscale(H)
    tab_words, tab_scales = pack_weight(n((K, T)) * s, "e4m3")
    w4_words, w4_scales = pack_weight(n((K, H)) * 0.8 / np.sqrt(K) / s, "e2m1")
    return {
        "tab_words": tab_words, "tab_scales": tab_scales,
        "offs": striped(np.random.permutation(T)[:S]),
        "pos1": striped(np.random.permutation(S)[:P]),
        "pos2": striped(np.random.permutation(S)[:P]),
        "w4_words": w4_words, "w4_scales": w4_scales,
        "w1": (n((K, H)) * 0.7 / np.sqrt(K) / s).astype(np.float32),
        "patch": (n((H, S)) * 0.7).astype(np.float32),
        "gain": (np.exp(0.3 * n(H)) * u).astype(np.float32),
        "side": (n(H) * 0.6 * u).astype(np.float32),
        "trait": (n(H) * 2.5 / np.sqrt(H) / u ** 2).astype(np.float32),
        "matchup": (n((P, P)) * 1.2).astype(np.float32),
    }


def reference(tab_words, tab_scales, offs, pos1, pos2, w4_words, w4_scales, w1, patch, gain, side, trait, matchup):
    v = unpack_weight(tab_words, tab_scales, "e4m3")[:, unstriped(offs)]
    w4 = unpack_weight(w4_words, w4_scales, "e2m1")
    w1q = mxq(f64(w1), 0, "e4m3")
    y = w4.T @ v + w1q.T @ v
    h = f64(gain)[:, None] * np.tanh(y + f64(patch))
    x1 = h[:, unstriped(pos1)]
    x2 = (h[:, unstriped(pos2)] + f64(side)[:, None]) * f64(trait)[:, None]
    e = mxq(x1, 0, "e4m3").T @ mxq(x2, 0, "e4m3")
    return 1.0 / (1.0 + np.exp(-(e + f64(matchup))))

@@ -1,0 +1,275 @@
+from contextlib import ExitStack
+
+import concourse.mybir as mybir
+from concourse.masks import make_identity
+
+K, H, T, S, P = 1024, 1024, 4096, 1024, 512
+FLOPS = 2 * (2 * K * H * S) + 2 * H * P * P
+
+F32 = mybir.dt.float32
+BF16 = mybir.dt.bfloat16
+I32 = mybir.dt.int32
+U32 = mybir.dt.uint32
+U16 = mybir.dt.uint16
+U8 = mybir.dt.uint8
+FP8X4 = mybir.dt.float8_e4m3fn_x4
+FP4X4 = mybir.dt.float4_e2m1fn_x4
+ACT = mybir.ActivationFunctionType
+ALU = mybir.AluOpType
+
+PARTS = 128
+PASS = 512
+BANK = 512
+BANKS = 8
+
+
+def tile_list_fighter_matchup_chart_kernel(
+    tc, tab_words, tab_scales, offs, pos1, pos2, w4_words, w4_scales, w1, patch, gain, side, trait, matchup, out
+):
+    nc = tc.nc
+    with ExitStack() as ctx:
+        keep = ctx.enter_context(tc.tile_pool(name="keep", bufs=1))
+        ring = ctx.enter_context(tc.tile_pool(name="ring", bufs=2))
+        psum = ctx.enter_context(tc.psum_pool(name="psum", bufs=1))
+
+        def kept(shape, dtype, name):
+            return keep.tile(shape, dtype, name=name, align_bytes=64)
+
+        def bank(n, name):
+            return psum.tile([PARTS, BANK], F32, name=name, tag="bank%d" % n)
+
+        offs_sb = keep.tile([PARTS, S // 16], U16, name="offs_sb")
+        pos1_sb = keep.tile([PARTS, P // 16], U16, name="pos1_sb")
+        pos2_sb = keep.tile([PARTS, P // 16], U16, name="pos2_sb")
+
+        tab_sc = kept([PARTS, T], U8, "tab_sc")
+        tab_w = [kept([PARTS, T], I32, "tab_w%d" % a) for a in range(2)]
+        v_sc_rows = kept([PARTS, S], U8, "v_sc_rows")
+        v_sc = kept([PARTS, 2, S], U8, "v_sc")
+        v_w = [kept([PARTS, S], U32, "v_w%d" % a) for a in range(2)]
+        w4_raw = kept([PARTS, 2, 2 * H], U8, "w4_raw")
+        w4_w = kept([PARTS, 2, 2 * H], U8, "w4_w")
+        w4_sc_raw = kept([PARTS, 2, H], U8, "w4_sc_raw")
+        w4_sc = kept([PARTS, 2, H], U8, "w4_sc")
+        vec_raw = kept([PARTS, H], F32, "vec_raw")
+        vec_rows = kept([PARTS, H], F32, "vec_rows")
+        ident = kept([PARTS, PARTS], F32, "ident")
+        vecs = kept([PARTS, 8, 3], F32, "vecs")
+        x2_mul = kept([PARTS, 8], F32, "x2_mul")
+        x2_add = kept([PARTS, 8], F32, "x2_add")
+
+        nc.vector.memset(tab_sc[32:64, :].bitcast(I32), 0)
+        nc.vector.memset(tab_sc[64:128, :].bitcast(I32), 0)
+        nc.gpsimd.memset(vec_rows[:], 0.0)
+        nc.gpsimd.memset(v_sc[:].rearrange("p a c -> p (a c)").bitcast(I32), 0)
+        nc.gpsimd.memset(w4_sc[:].rearrange("p a c -> p (a c)").bitcast(I32), 0)
+        make_identity(nc, ident[:])
+
+        nc.sync.dma_start(offs_sb[:], offs)
+        nc.sync.dma_start(tab_sc[0:32, :].bitcast(I32), tab_scales.bitcast(I32).rearrange("a q c -> q a c"))
+        for n, vec in enumerate((gain, side, trait)):
+            nc.sync.dma_start(vec_raw[n : n + 1, :], vec.rearrange("(o r) -> o r", o=1))
+        nc.sync.dma_start(tab_w[0][:], tab_words[0].rearrange("p t i -> p (t i)").bitcast(I32))
+        for q in range(4):
+            nc.sync.dma_start(
+                w4_sc_raw[32 * q : 32 * q + 4].bitcast(I32),
+                w4_scales.bitcast(I32)[:, 4 * q : 4 * q + 4, :].rearrange("a q c -> q a c"),
+            )
+        nc.sync.dma_start(w4_raw[:].bitcast(I32), w4_words.bitcast(I32).rearrange("a p c -> p a c"))
+        nc.sync.dma_start(tab_w[1][:], tab_words[1].rearrange("p t i -> p (t i)").bitcast(I32))
+
+        nc.sync.dma_start(pos2_sb[:], pos2)
+        nc.vector.tensor_copy(v_sc_rows[:], tab_sc[:].indirect(offs_sb[:]))
+        for q in range(4):
+            nc.sync.dma_start(
+                v_sc[32 * q : 32 * q + 4].rearrange("p a c -> p (a c)").bitcast(I32),
+                v_sc_rows[8 * q : 8 * q + 8, :].bitcast(I32),
+            )
+
+        w1_raw = {}
+        z = {}
+
+        def load_w1(b, a):
+            w1_raw[b, a] = kept([PARTS, 4, PASS], F32, "w1_raw%d%d" % (b, a))
+            rows = w1[PASS * a : PASS * (a + 1), PASS * b : PASS * (b + 1)]
+            nc.sync.dma_start(w1_raw[b, a][:], rows.rearrange("(p j) c -> p j c", j=4))
+
+        def load_patch(b, t):
+            z[b, t] = kept([PARTS, S], F32, "z%d%d" % (b, t))
+            rows = patch[PASS * b : PASS * (b + 1), :].rearrange("(g t i) c -> t g i c", t=4, i=8)
+            nc.sync.dma_start(z[b, t][:], rows[t])
+
+        for b in range(2):
+            for a in range(2):
+                load_w1(b, a)
+            for t in range(4):
+                load_patch(b, t)
+                if (b, t) == (0, 0):
+                    nc.sync.dma_start(pos1_sb[:], pos1)
+        res = []
+        for i in range(4):
+            res.append(kept([PARTS, P], F32, "res%d" % i))
+            nc.sync.dma_start(res[i][:], matchup[PARTS * i : PARTS * (i + 1), :])
+
+        nc.vector.tensor_copy(
+            w4_w[:].rearrange("p a c -> p (a c)").bitcast(I32).rearrange("p (n t g w) -> p n t g w", n=4, t=4, w=4),
+            w4_raw[:].rearrange("p a c -> p (a c)").bitcast(I32).rearrange("p (n g t w) -> p n t g w", n=4, t=4, w=4),
+        )
+        nc.vector.tensor_copy(v_w[0][:], tab_w[0][:].bitcast(U32).indirect(offs_sb[:]))
+        for q in range(4):
+            rows = slice(32 * q, 32 * q + 4)
+            nc.vector.tensor_copy(
+                w4_sc[rows].rearrange("p a c -> p (a c)").bitcast(I32).rearrange("p (n t g w) -> p n t g w", n=4, t=4, w=2),
+                w4_sc_raw[rows].rearrange("p a c -> p (a c)").bitcast(I32).rearrange("p (n g t w) -> p n t g w", n=4, t=4, w=2),
+            )
+        nc.vector.tensor_copy(v_w[1][:], tab_w[1][:].bitcast(U32).indirect(offs_sb[:]))
+
+        def spread_vectors():
+            nc.scalar.copy(
+                vec_rows[0:3, :].rearrange("v (b t g i) -> v b t g i", b=2, t=4, i=8),
+                vec_raw[0:3, :].rearrange("v (b g t i) -> v b t g i", b=2, t=4, i=8),
+            )
+            for b in range(2):
+                vec_ps = bank(BANKS - 2 + b, "vec_ps")
+                for t in range(4):
+                    s = 4 * b + t
+                    nc.tensor.transpose(vec_ps[:, PARTS * t : PARTS * (t + 1)], vec_rows[:, PARTS * s : PARTS * (s + 1)], ident[:])
+                nc.scalar.copy(vecs[:, 4 * b : 4 * b + 4, :], vec_ps[:].rearrange("p (t c) -> p t c", t=4)[:, :, 0:3])
+            nc.gpsimd.tensor_tensor(x2_mul[:], vecs[:, :, 0], vecs[:, :, 2], ALU.mult)
+            nc.gpsimd.tensor_tensor(x2_add[:], vecs[:, :, 1], vecs[:, :, 2], ALU.mult)
+
+        spread_vectors()
+        w1_w = {}
+        w1_sc = {}
+        w1_bf = {}
+
+        def round_w1(b, a, t, engine):
+            if t == 0:
+                w1_bf[b, a] = ring.tile([PARTS, 4, PASS], BF16, name="w1_bf", align_bytes=64)
+                w1_w[b, a] = kept([PARTS, PASS], U32, "w1_w%d%d" % (b, a))
+                w1_sc[b, a] = kept([PARTS, PASS], U8, "w1_sc%d%d" % (b, a))
+            src = w1_raw[b, a][:].rearrange("p j (g t i) -> p t g j i", t=4, i=8)[:, t]
+            dst = w1_bf[b, a][:, t, :].rearrange("p (g i j) -> p g j i", i=8, j=4)
+            if engine == "vector":
+                nc.vector.tensor_copy(dst, src)
+            else:
+                nc.scalar.copy(dst, src)
+
+        def quantize_w1(b, a, t0, t1):
+            cols = slice(PARTS * t0, PARTS * t1)
+            nc.vector.quantize_mx(
+                out=w1_w[b, a][:, cols].bitcast(FP8X4),
+                scales=w1_sc[b, a][:, cols],
+                in_=w1_bf[b, a][:, t0:t1, :].rearrange("p t c -> p (t c)"),
+            )
+
+        for t in range(4):
+            round_w1(0, 0, t, "scalar")
+        quantize_w1(0, 0, 0, 4)
+        for t in range(4):
+            round_w1(0, 1, t, "vector" if t == 0 else "scalar")
+            quantize_w1(0, 1, t, t + 1)
+
+        def features(s):
+            b, t = divmod(s, 4)
+            for half in range(2):
+                acc = bank((2 * s + half) % 6, "y_ps")
+                cols = slice(BANK * half, BANK * (half + 1))
+                for a in range(2):
+                    c0 = PASS * b + PARTS * t
+                    nc.tensor.matmul_mx(
+                        out=acc[:],
+                        lhsT=w4_w[:, a, 2 * c0 : 2 * (c0 + PARTS)].bitcast(FP4X4),
+                        lhsT_scale=w4_sc[:, a, c0 : c0 + PARTS],
+                        rhs=v_w[a][:, cols].bitcast(FP8X4),
+                        rhs_scale=v_sc[:, a, cols],
+                        start=(a == 0),
+                        stop=False,
+                    )
+                for a in range(2):
+                    nc.tensor.matmul_mx(
+                        out=acc[:],
+                        lhsT=w1_w[b, a][:, PARTS * t : PARTS * (t + 1)].bitcast(FP8X4),
+                        lhsT_scale=w1_sc[b, a][:, PARTS * t : PARTS * (t + 1)],
+                        rhs=v_w[a][:, cols].bitcast(FP8X4),
+                        rhs_scale=v_sc[:, a, cols],
+                        start=False,
+                        stop=(a == 1),
+                    )
+                nc.vector.tensor_tensor(z[b, t][:, cols], acc[:], z[b, t][:, cols], ALU.add)
+                nc.scalar.activation(z[b, t][:, cols], z[b, t][:, cols], ACT.Tanh)
+
+        x1_rows = [kept([PARTS, 2, P, 2], BF16, "x1_rows%d" % b) for b in range(2)]
+        x2_rows = [kept([PARTS, 2, P, 2], BF16, "x2_rows%d" % b) for b in range(2)]
+
+        def pick(s):
+            b, t = divmod(s, 4)
+            g2 = ring.tile([PARTS, P], F32, name="g2")
+            g1 = ring.tile([PARTS, P], F32, name="g1")
+            nc.vector.tensor_copy(g2[:], z[b, t][:].indirect(pos2_sb[:]))
+            nc.scalar.activation(x2_rows[b][:, t // 2, :, t % 2], g2[:], ACT.Identity, bias=x2_add[:, s : s + 1], scale=x2_mul[:, s : s + 1])
+            nc.vector.tensor_copy(g1[:], z[b, t][:].indirect(pos1_sb[:]))
+            nc.scalar.activation(x1_rows[b][:, t // 2, :, t % 2], g1[:], ACT.Copy, scale=vecs[:, s, 0:1])
+
+        x1_bf = [kept([PARTS, 4 * P], BF16, "x1_bf%d" % b) for b in range(2)]
+        x2_bf = [kept([PARTS, 4 * P], BF16, "x2_bf%d" % b) for b in range(2)]
+        x1_w = [kept([PARTS, P], U32, "x1_w%d" % b) for b in range(2)]
+        x2_w = [kept([PARTS, P], U32, "x2_w%d" % b) for b in range(2)]
+        x1_sc = [kept([PARTS, P], U8, "x1_sc%d" % b) for b in range(2)]
+        x2_sc = [kept([PARTS, P], U8, "x2_sc%d" % b) for b in range(2)]
+
+        def weave(dst, rows, c0, c1, engine):
+            src = rows[:].rearrange("p u c e -> p u (c e)").bitcast(U32 if engine == "scalar" else I32)[:, :, c0:c1].rearrange("p u (c i) -> p c u i", i=4)
+            dstv = dst[:].bitcast(U32 if engine == "scalar" else I32)[:, 2 * c0 : 2 * c1].rearrange("p (c i u) -> p c u i", i=4, u=2)
+            if engine == "vector":
+                nc.vector.tensor_copy(dstv, src)
+            else:
+                nc.scalar.copy(dstv, src)
+
+        def quantize_x(words, scales, src, c0, c1):
+            nc.vector.quantize_mx(out=words[:, c0:c1].bitcast(FP8X4), scales=scales[:, c0:c1], in_=src[:, 4 * c0 : 4 * c1])
+
+        e_ps = {}
+
+        def score(b, i):
+            if b == 0:
+                e_ps[i] = bank((6, 7, 4, 5)[i], "e_ps")
+            rows = slice(PARTS * i, PARTS * (i + 1))
+            nc.tensor.matmul_mx(
+                out=e_ps[i][:],
+                lhsT=x1_w[b][:, rows].bitcast(FP8X4),
+                lhsT_scale=x1_sc[b][:, rows],
+                rhs=x2_w[b][:].bitcast(FP8X4),
+                rhs_scale=x2_sc[b][:],
+                start=(b == 0),
+                stop=(b == 1),
+            )
+
+        for s in range(8):
+            features(s)
+            if s > 0:
+                pick(s - 1)
+            if s in (1, 2):
+                for t in range(4):
+                    round_w1(1, s - 1, t, "scalar")
+                quantize_w1(1, s - 1, 0, 4)
+            if s == 4:
+                weave(x2_bf[0], x2_rows[0], 0, P, "scalar")
+                quantize_x(x2_w[0], x2_sc[0], x2_bf[0], 0, P)
+            if s == 5:
+                weave(x1_bf[0], x1_rows[0], 0, P, "scalar")
+                quantize_x(x1_w[0], x1_sc[0], x1_bf[0], 0, P)
+        for i in range(4):
+            score(0, i)
+        pick(7)
+        weave(x2_bf[1], x2_rows[1], 0, P, "vector")
+        for i in range(4):
+            weave(x1_bf[1], x1_rows[1], PARTS * i, PARTS * (i + 1), "scalar")
+        quantize_x(x2_w[1], x2_sc[1], x2_bf[1], 0, P)
+        for i in range(4):
+            quantize_x(x1_w[1], x1_sc[1], x1_bf[1], PARTS * i, PARTS * (i + 1))
+            score(1, i)
+        for i in range(4):
+            nc.vector.tensor_tensor(res[i][:], e_ps[i][:], res[i][:], ALU.add)
+            nc.scalar.activation(res[i][:], res[i][:], ACT.Sigmoid)
+            nc.sync.dma_start(out[PARTS * i : PARTS * (i + 1), :], res[i][:])

@@ -122,14 +122,20 @@ def tile_list_fighter_matchup_chart_kernel(
                 w4_sc[rows].rearrange("p a c -> p (a c)").bitcast(I32).rearrange("p (n t g w) -> p n t g w", n=4, t=4, w=2),
                 w4_sc_raw[rows].rearrange("p a c -> p (a c)").bitcast(I32).rearrange("p (n g t w) -> p n t g w", n=4, t=4, w=2),
             )
-        nc.vector.tensor_copy(v_w[1][:], tab_w[1][:].bitcast(U32).indirect(offs_sb[:]))
+        for half in range(2):
+            nc.vector.tensor_copy(
+                v_w[1][:, BANK * half : BANK * (half + 1)],
+                tab_w[1][:].bitcast(U32).indirect(offs_sb[:, BANK // 16 * half : BANK // 16 * (half + 1)]),
+            )
 
         def spread_vectors():
-            nc.scalar.copy(
-                vec_rows[0:3, :].rearrange("v (b t g i) -> v b t g i", b=2, t=4, i=8),
-                vec_raw[0:3, :].rearrange("v (b g t i) -> v b t g i", b=2, t=4, i=8),
-            )
             for b in range(2):
+                cols = slice(PASS * b, PASS * (b + 1))
+                nc.scalar.activation(
+                    vec_rows[0:3, cols].rearrange("v (t g i) -> v t g i", t=4, i=8),
+                    vec_raw[0:3, cols].rearrange("v (g t i) -> v t g i", t=4, i=8),
+                    ACT.Copy,
+                )
                 vec_ps = bank(BANKS - 2 + b, "vec_ps")
                 for t in range(4):
                     s = 4 * b + t
@@ -148,8 +154,8 @@ def tile_list_fighter_matchup_chart_kernel(
                 w1_bf[b, a] = ring.tile([PARTS, 4, PASS], BF16, name="w1_bf", align_bytes=64)
                 w1_w[b, a] = kept([PARTS, PASS], U32, "w1_w%d%d" % (b, a))
                 w1_sc[b, a] = kept([PARTS, PASS], U8, "w1_sc%d%d" % (b, a))
-            src = w1_raw[b, a][:].rearrange("p j (g t i) -> p t g j i", t=4, i=8)[:, t]
-            dst = w1_bf[b, a][:, t, :].rearrange("p (g i j) -> p g j i", i=8, j=4)
+            src = w1_raw[b, a][:].rearrange("p j (g t u i) -> p t g u j i", t=4, u=2, i=4)[:, t]
+            dst = w1_bf[b, a][:, t, :].rearrange("p (g u i j) -> p g u j i", u=2, i=4, j=4)
             if engine == "vector":
                 nc.vector.tensor_copy(dst, src)
             else:
@@ -164,8 +170,9 @@ def tile_list_fighter_matchup_chart_kernel(
             )
 
         for t in range(4):
-            round_w1(0, 0, t, "scalar")
-        quantize_w1(0, 0, 0, 4)
+            round_w1(0, 0, t, "vector" if t < 2 else "scalar")
+        for t in range(4):
+            quantize_w1(0, 0, t, t + 1)
         for t in range(4):
             round_w1(0, 1, t, "vector" if t == 0 else "scalar")
             quantize_w1(0, 1, t, t + 1)
@@ -173,7 +180,7 @@ def tile_list_fighter_matchup_chart_kernel(
         def features(s):
             b, t = divmod(s, 4)
             for half in range(2):
-                acc = bank((2 * s + half) % 6, "y_ps")
+                acc = bank((2 * s + half) % 4, "y_ps")
                 cols = slice(BANK * half, BANK * (half + 1))
                 for a in range(2):
                     c0 = PASS * b + PARTS * t
@@ -202,14 +209,21 @@ def tile_list_fighter_matchup_chart_kernel(
         x1_rows = [kept([PARTS, 2, P, 2], BF16, "x1_rows%d" % b) for b in range(2)]
         x2_rows = [kept([PARTS, 2, P, 2], BF16, "x2_rows%d" % b) for b in range(2)]
 
-        def pick(s):
+        def pick2(s):
             b, t = divmod(s, 4)
             g2 = ring.tile([PARTS, P], F32, name="g2")
-            g1 = ring.tile([PARTS, P], F32, name="g1")
             nc.vector.tensor_copy(g2[:], z[b, t][:].indirect(pos2_sb[:]))
             nc.scalar.activation(x2_rows[b][:, t // 2, :, t % 2], g2[:], ACT.Identity, bias=x2_add[:, s : s + 1], scale=x2_mul[:, s : s + 1])
-            nc.vector.tensor_copy(g1[:], z[b, t][:].indirect(pos1_sb[:]))
-            nc.scalar.activation(x1_rows[b][:, t // 2, :, t % 2], g1[:], ACT.Copy, scale=vecs[:, s, 0:1])
+
+        def pick1(s, c0, c1):
+            b, t = divmod(s, 4)
+            g1 = ring.tile([PARTS, c1 - c0], F32, name="g1", bufs=4)
+            nc.vector.tensor_copy(g1[:], z[b, t][:].indirect(pos1_sb[:, c0 // 16 : c1 // 16]))
+            dst = x1_rows[b][:, t // 2, c0:c1, t % 2]
+            if s < 6:
+                nc.gpsimd.tensor_scalar(dst, g1[:], vecs[:, s, 0:1], 0.0, ALU.mult, ALU.add)
+            else:
+                nc.scalar.activation(dst, g1[:], ACT.Copy, scale=vecs[:, s, 0:1])
 
         x1_bf = [kept([PARTS, 4 * P], BF16, "x1_bf%d" % b) for b in range(2)]
         x2_bf = [kept([PARTS, 4 * P], BF16, "x2_bf%d" % b) for b in range(2)]
@@ -233,7 +247,7 @@ def tile_list_fighter_matchup_chart_kernel(
 
         def score(b, i):
             if b == 0:
-                e_ps[i] = bank((6, 7, 4, 5)[i], "e_ps")
+                e_ps[i] = bank(4 + i, "e_ps")
             rows = slice(PARTS * i, PARTS * (i + 1))
             nc.tensor.matmul_mx(
                 out=e_ps[i][:],
@@ -248,7 +262,8 @@ def tile_list_fighter_matchup_chart_kernel(
         for s in range(8):
             features(s)
             if s > 0:
-                pick(s - 1)
+                pick2(s - 1)
+                pick1(s - 1, 0, P)
             if s in (1, 2):
                 for t in range(4):
                     round_w1(1, s - 1, t, "scalar")
@@ -261,15 +276,19 @@ def tile_list_fighter_matchup_chart_kernel(
                 quantize_x(x1_w[0], x1_sc[0], x1_bf[0], 0, P)
         for i in range(4):
             score(0, i)
-        pick(7)
-        weave(x2_bf[1], x2_rows[1], 0, P, "vector")
+        pick2(7)
         for i in range(4):
+            pick1(7, PARTS * i, PARTS * (i + 1))
             weave(x1_bf[1], x1_rows[1], PARTS * i, PARTS * (i + 1), "scalar")
+        weave(x2_bf[1], x2_rows[1], 0, P, "vector")
+        quantize_x(x1_w[1], x1_sc[1], x1_bf[1], 0, PARTS)
         quantize_x(x2_w[1], x2_sc[1], x2_bf[1], 0, P)
         for i in range(4):
-            quantize_x(x1_w[1], x1_sc[1], x1_bf[1], PARTS * i, PARTS * (i + 1))
+            if i > 0:
+                quantize_x(x1_w[1], x1_sc[1], x1_bf[1], PARTS * i, PARTS * (i + 1))
             score(1, i)
         for i in range(4):
-            nc.vector.tensor_tensor(res[i][:], e_ps[i][:], res[i][:], ALU.add)
-            nc.scalar.activation(res[i][:], res[i][:], ACT.Sigmoid)
-            nc.sync.dma_start(out[PARTS * i : PARTS * (i + 1), :], res[i][:])
+            for c0, c1 in ((0, P),) if i < 3 else ((0, P // 2), (P // 2, P)):
+                nc.vector.tensor_tensor(res[i][:, c0:c1], e_ps[i][:, c0:c1], res[i][:, c0:c1], ALU.add)
+                nc.scalar.activation(res[i][:, c0:c1], res[i][:, c0:c1], ACT.Sigmoid)
+                nc.sync.dma_start(out[PARTS * i : PARTS * (i + 1), c0:c1], res[i][:, c0:c1])

@@ -1,7 +1,6 @@
 from contextlib import ExitStack
 
 import concourse.mybir as mybir
-from concourse.masks import make_identity
 
 K, H, T, S, P = 1024, 1024, 4096, 1024, 512
 FLOPS = 2 * (2 * K * H * S) + 2 * H * P * P
@@ -51,34 +50,31 @@ def tile_list_fighter_matchup_chart_kernel(
         w4_w = kept([PARTS, 2, 2 * H], U8, "w4_w")
         w4_sc_raw = kept([PARTS, 2, H], U8, "w4_sc_raw")
         w4_sc = kept([PARTS, 2, H], U8, "w4_sc")
-        vec_raw = kept([PARTS, H], F32, "vec_raw")
-        vec_rows = kept([PARTS, H], F32, "vec_rows")
-        ident = kept([PARTS, PARTS], F32, "ident")
-        vecs = kept([PARTS, 8, 3], F32, "vecs")
-        x2_mul = kept([PARTS, 8], F32, "x2_mul")
-        x2_add = kept([PARTS, 8], F32, "x2_add")
+        gain_sb, side_sb, trait_sb = [kept([PARTS, 2, 8], F32, name) for name in ("gain_sb", "side_sb", "trait_sb")]
+        warm = kept([PARTS, 1], F32, "warm")
+        x2_mul = kept([PARTS, 2, 4], F32, "x2_mul")
+        x2_add = kept([PARTS, 2, 4], F32, "x2_add")
 
-        nc.vector.memset(tab_sc[32:64, :].bitcast(I32), 0)
+        nc.vector.memset(w4_sc_raw[:].rearrange("p a c -> p (a c)").bitcast(I32), 0)
         nc.vector.memset(tab_sc[64:128, :].bitcast(I32), 0)
-        nc.gpsimd.memset(vec_rows[:], 0.0)
+        nc.gpsimd.memset(warm[:], 0.0)
+        nc.gpsimd.memset(tab_sc[32:64, :].bitcast(I32), 0)
         nc.gpsimd.memset(v_sc[:].rearrange("p a c -> p (a c)").bitcast(I32), 0)
-        nc.gpsimd.memset(w4_sc[:].rearrange("p a c -> p (a c)").bitcast(I32), 0)
-        make_identity(nc, ident[:])
+        nc.scalar.activation(warm[:], warm[:], ACT.Sigmoid)
 
         nc.sync.dma_start(offs_sb[:], offs)
         nc.sync.dma_start(tab_sc[0:32, :].bitcast(I32), tab_scales.bitcast(I32).rearrange("a q c -> q a c"))
-        for n, vec in enumerate((gain, side, trait)):
-            nc.sync.dma_start(vec_raw[n : n + 1, :], vec.rearrange("(o r) -> o r", o=1))
+        for vec_sb, vec in ((gain_sb, gain), (side_sb, side), (trait_sb, trait)):
+            nc.sync.dma_start(vec_sb[:, :, 0:4], vec.rearrange("(b p t) -> p b t", b=2, t=4))
         nc.sync.dma_start(tab_w[0][:], tab_words[0].rearrange("p t i -> p (t i)").bitcast(I32))
+        nc.sync.dma_start(w4_raw[:].bitcast(I32), w4_words.bitcast(I32).rearrange("a p c -> p a c"))
+        nc.sync.dma_start(pos2_sb[:], pos2)
         for q in range(4):
             nc.sync.dma_start(
                 w4_sc_raw[32 * q : 32 * q + 4].bitcast(I32),
                 w4_scales.bitcast(I32)[:, 4 * q : 4 * q + 4, :].rearrange("a q c -> q a c"),
             )
-        nc.sync.dma_start(w4_raw[:].bitcast(I32), w4_words.bitcast(I32).rearrange("a p c -> p a c"))
         nc.sync.dma_start(tab_w[1][:], tab_words[1].rearrange("p t i -> p (t i)").bitcast(I32))
-
-        nc.sync.dma_start(pos2_sb[:], pos2)
         nc.vector.tensor_copy(v_sc_rows[:], tab_sc[:].indirect(offs_sb[:]))
         for q in range(4):
             nc.sync.dma_start(
@@ -96,66 +92,54 @@ def tile_list_fighter_matchup_chart_kernel(
 
         def load_patch(b, t):
             z[b, t] = kept([PARTS, S], F32, "z%d%d" % (b, t))
-            rows = patch[PASS * b : PASS * (b + 1), :].rearrange("(g t i) c -> t g i c", t=4, i=8)
+            rows = patch[PASS * b : PASS * (b + 1), :].rearrange("(p t) c -> t p c", t=4)
             nc.sync.dma_start(z[b, t][:], rows[t])
 
-        for b in range(2):
-            for a in range(2):
-                load_w1(b, a)
-            for t in range(4):
-                load_patch(b, t)
-                if (b, t) == (0, 0):
-                    nc.sync.dma_start(pos1_sb[:], pos1)
+        load_w1(0, 0)
+        load_w1(0, 1)
+        load_patch(0, 0)
+        nc.sync.dma_start(pos1_sb[:], pos1)
+        load_patch(0, 1)
+        load_patch(0, 2)
+        load_w1(1, 0)
+        load_patch(0, 3)
+        load_w1(1, 1)
+        for t in range(4):
+            load_patch(1, t)
         res = []
         for i in range(4):
             res.append(kept([PARTS, P], F32, "res%d" % i))
             nc.sync.dma_start(res[i][:], matchup[PARTS * i : PARTS * (i + 1), :])
 
-        nc.vector.tensor_copy(
-            w4_w[:].rearrange("p a c -> p (a c)").bitcast(I32).rearrange("p (n t g w) -> p n t g w", n=4, t=4, w=4),
-            w4_raw[:].rearrange("p a c -> p (a c)").bitcast(I32).rearrange("p (n g t w) -> p n t g w", n=4, t=4, w=4),
-        )
         nc.vector.tensor_copy(v_w[0][:], tab_w[0][:].bitcast(U32).indirect(offs_sb[:]))
-        for q in range(4):
-            rows = slice(32 * q, 32 * q + 4)
-            nc.vector.tensor_copy(
-                w4_sc[rows].rearrange("p a c -> p (a c)").bitcast(I32).rearrange("p (n t g w) -> p n t g w", n=4, t=4, w=2),
-                w4_sc_raw[rows].rearrange("p a c -> p (a c)").bitcast(I32).rearrange("p (n g t w) -> p n t g w", n=4, t=4, w=2),
-            )
+        nc.vector.tensor_copy(
+            w4_w[:].rearrange("p a c -> p (a c)").bitcast(U16).rearrange("p (n t m) -> p n t m", n=4, t=4),
+            w4_raw[:].rearrange("p a c -> p (a c)").bitcast(U16).rearrange("p (n m t) -> p n t m", n=4, t=4),
+        )
+        nc.vector.tensor_copy(
+            w4_sc[:].rearrange("p a (b t m) -> p (a b) t m", b=2, t=4),
+            w4_sc_raw[:].rearrange("p a (b m t) -> p (a b) t m", b=2, t=4),
+        )
         for half in range(2):
             nc.vector.tensor_copy(
                 v_w[1][:, BANK * half : BANK * (half + 1)],
                 tab_w[1][:].bitcast(U32).indirect(offs_sb[:, BANK // 16 * half : BANK // 16 * (half + 1)]),
             )
 
-        def spread_vectors():
-            for b in range(2):
-                cols = slice(PASS * b, PASS * (b + 1))
-                nc.scalar.activation(
-                    vec_rows[0:3, cols].rearrange("v (t g i) -> v t g i", t=4, i=8),
-                    vec_raw[0:3, cols].rearrange("v (g t i) -> v t g i", t=4, i=8),
-                    ACT.Copy,
-                )
-                vec_ps = bank(BANKS - 2 + b, "vec_ps")
-                for t in range(4):
-                    s = 4 * b + t
-                    nc.tensor.transpose(vec_ps[:, PARTS * t : PARTS * (t + 1)], vec_rows[:, PARTS * s : PARTS * (s + 1)], ident[:])
-                nc.scalar.copy(vecs[:, 4 * b : 4 * b + 4, :], vec_ps[:].rearrange("p (t c) -> p t c", t=4)[:, :, 0:3])
-            nc.gpsimd.tensor_tensor(x2_mul[:], vecs[:, :, 0], vecs[:, :, 2], ALU.mult)
-            nc.gpsimd.tensor_tensor(x2_add[:], vecs[:, :, 1], vecs[:, :, 2], ALU.mult)
+        nc.gpsimd.tensor_tensor(x2_mul[:], gain_sb[:, :, 0:4], trait_sb[:, :, 0:4], ALU.mult)
+        nc.gpsimd.tensor_tensor(x2_add[:], side_sb[:, :, 0:4], trait_sb[:, :, 0:4], ALU.mult)
 
-        spread_vectors()
         w1_w = {}
         w1_sc = {}
         w1_bf = {}
 
-        def round_w1(b, a, t, engine):
-            if t == 0:
+        def round_w1(b, a, u, engine):
+            if u == 0:
                 w1_bf[b, a] = ring.tile([PARTS, 4, PASS], BF16, name="w1_bf", align_bytes=64)
                 w1_w[b, a] = kept([PARTS, PASS], U32, "w1_w%d%d" % (b, a))
                 w1_sc[b, a] = kept([PARTS, PASS], U8, "w1_sc%d%d" % (b, a))
-            src = w1_raw[b, a][:].rearrange("p j (g t u i) -> p t g u j i", t=4, u=2, i=4)[:, t]
-            dst = w1_bf[b, a][:, t, :].rearrange("p (g u i j) -> p g u j i", u=2, i=4, j=4)
+            src = w1_raw[b, a][:].rearrange("p j (m t) -> p m j t", t=4)[:, :, :, 2 * u : 2 * u + 2]
+            dst = w1_bf[b, a][:, 2 * u : 2 * u + 2, :].rearrange("p t (m j) -> p m j t", j=4)
             if engine == "vector":
                 nc.vector.tensor_copy(dst, src)
             else:
@@ -169,13 +153,12 @@ def tile_list_fighter_matchup_chart_kernel(
                 in_=w1_bf[b, a][:, t0:t1, :].rearrange("p t c -> p (t c)"),
             )
 
-        for t in range(4):
-            round_w1(0, 0, t, "vector" if t < 2 else "scalar")
-        for t in range(4):
-            quantize_w1(0, 0, t, t + 1)
-        for t in range(4):
-            round_w1(0, 1, t, "vector" if t == 0 else "scalar")
-            quantize_w1(0, 1, t, t + 1)
+        for a in range(2):
+            round_w1(0, a, 0, "vector")
+            round_w1(0, a, 1, "scalar")
+            quantize_w1(0, a, 0, 1)
+            quantize_w1(0, a, 1, 2)
+            quantize_w1(0, a, 2, 4)
 
         def features(s):
             b, t = divmod(s, 4)
@@ -213,7 +196,7 @@ def tile_list_fighter_matchup_chart_kernel(
             b, t = divmod(s, 4)
             g2 = ring.tile([PARTS, P], F32, name="g2")
             nc.vector.tensor_copy(g2[:], z[b, t][:].indirect(pos2_sb[:]))
-            nc.scalar.activation(x2_rows[b][:, t // 2, :, t % 2], g2[:], ACT.Identity, bias=x2_add[:, s : s + 1], scale=x2_mul[:, s : s + 1])
+            nc.scalar.activation(x2_rows[b][:, t // 2, :, t % 2], g2[:], ACT.Identity, bias=x2_add[:, b, t : t + 1], scale=x2_mul[:, b, t : t + 1])
 
         def pick1(s, c0, c1):
             b, t = divmod(s, 4)
@@ -221,9 +204,9 @@ def tile_list_fighter_matchup_chart_kernel(
             nc.vector.tensor_copy(g1[:], z[b, t][:].indirect(pos1_sb[:, c0 // 16 : c1 // 16]))
             dst = x1_rows[b][:, t // 2, c0:c1, t % 2]
             if s < 6:
-                nc.gpsimd.tensor_scalar(dst, g1[:], vecs[:, s, 0:1], 0.0, ALU.mult, ALU.add)
+                nc.gpsimd.tensor_scalar(dst, g1[:], gain_sb[:, b, t : t + 1], 0.0, ALU.mult, ALU.add)
             else:
-                nc.scalar.activation(dst, g1[:], ACT.Copy, scale=vecs[:, s, 0:1])
+                nc.scalar.activation(dst, g1[:], ACT.Copy, scale=gain_sb[:, b, t : t + 1])
 
         x1_bf = [kept([PARTS, 4 * P], BF16, "x1_bf%d" % b) for b in range(2)]
         x2_bf = [kept([PARTS, 4 * P], BF16, "x2_bf%d" % b) for b in range(2)]
@@ -265,8 +248,8 @@ def tile_list_fighter_matchup_chart_kernel(
                 pick2(s - 1)
                 pick1(s - 1, 0, P)
             if s in (1, 2):
-                for t in range(4):
-                    round_w1(1, s - 1, t, "scalar")
+                for u in range(2):
+                    round_w1(1, s - 1, u, "scalar")
                 quantize_w1(1, s - 1, 0, 4)
             if s == 4:
                 weave(x2_bf[0], x2_rows[0], 0, P, "scalar")

from contextlib import ExitStack

import concourse.mybir as mybir

K, H, T, S, P = 1024, 1024, 4096, 1024, 512
FLOPS = 2 * (2 * K * H * S) + 2 * H * P * P

F32 = mybir.dt.float32
BF16 = mybir.dt.bfloat16
I32 = mybir.dt.int32
U32 = mybir.dt.uint32
U16 = mybir.dt.uint16
U8 = mybir.dt.uint8
FP8X4 = mybir.dt.float8_e4m3fn_x4
FP4X4 = mybir.dt.float4_e2m1fn_x4
ACT = mybir.ActivationFunctionType
ALU = mybir.AluOpType

PARTS = 128
PASS = 512
BANK = 512
BANKS = 8


def tile_list_fighter_matchup_chart_kernel(
    tc, tab_words, tab_scales, offs, pos1, pos2, w4_words, w4_scales, w1, patch, gain, side, trait, matchup, out
):
    nc = tc.nc
    with ExitStack() as ctx:
        keep = ctx.enter_context(tc.tile_pool(name="keep", bufs=1))
        ring = ctx.enter_context(tc.tile_pool(name="ring", bufs=2))
        psum = ctx.enter_context(tc.psum_pool(name="psum", bufs=1))

        def kept(shape, dtype, name):
            return keep.tile(shape, dtype, name=name, align_bytes=64)

        def bank(n, name):
            return psum.tile([PARTS, BANK], F32, name=name, tag="bank%d" % n)

        offs_sb = keep.tile([PARTS, S // 16], U16, name="offs_sb")
        pos1_sb = keep.tile([PARTS, P // 16], U16, name="pos1_sb")
        pos2_sb = keep.tile([PARTS, P // 16], U16, name="pos2_sb")

        tab_sc = kept([PARTS, T], U8, "tab_sc")
        tab_w = [kept([PARTS, T], I32, "tab_w%d" % a) for a in range(2)]
        v_sc_rows = kept([PARTS, S], U8, "v_sc_rows")
        v_sc = kept([PARTS, 2, S], U8, "v_sc")
        v_w = [kept([PARTS, S], U32, "v_w%d" % a) for a in range(2)]
        w4_raw = kept([PARTS, 2, 2 * H], U8, "w4_raw")
        w4_w = kept([PARTS, 2, 2 * H], U8, "w4_w")
        w4_sc_raw = kept([PARTS, 2, H], U8, "w4_sc_raw")
        w4_sc = kept([PARTS, 2, H], U8, "w4_sc")
        gain_sb, side_sb, trait_sb = [kept([PARTS, 2, 8], F32, name) for name in ("gain_sb", "side_sb", "trait_sb")]
        warm = kept([PARTS, 1], F32, "warm")
        x2_mul = kept([PARTS, 2, 4], F32, "x2_mul")
        x2_add = kept([PARTS, 2, 4], F32, "x2_add")

        nc.vector.memset(w4_sc_raw[:].rearrange("p a c -> p (a c)").bitcast(I32), 0)
        nc.vector.memset(tab_sc[64:128, :].bitcast(I32), 0)
        nc.gpsimd.memset(warm[:], 0.0)
        nc.gpsimd.memset(tab_sc[32:64, :].bitcast(I32), 0)
        nc.gpsimd.memset(v_sc[:].rearrange("p a c -> p (a c)").bitcast(I32), 0)
        nc.scalar.activation(warm[:], warm[:], ACT.Sigmoid)

        nc.sync.dma_start(offs_sb[:], offs)
        nc.sync.dma_start(tab_sc[0:32, :].bitcast(I32), tab_scales.bitcast(I32).rearrange("a q c -> q a c"))
        for vec_sb, vec in ((gain_sb, gain), (side_sb, side), (trait_sb, trait)):
            nc.sync.dma_start(vec_sb[:, :, 0:4], vec.rearrange("(b p t) -> p b t", b=2, t=4))
        nc.sync.dma_start(tab_w[0][:], tab_words[0].rearrange("p t i -> p (t i)").bitcast(I32))
        nc.sync.dma_start(w4_raw[:].bitcast(I32), w4_words.bitcast(I32).rearrange("a p c -> p a c"))
        nc.sync.dma_start(pos2_sb[:], pos2)
        for q in range(4):
            nc.sync.dma_start(
                w4_sc_raw[32 * q : 32 * q + 4].bitcast(I32),
                w4_scales.bitcast(I32)[:, 4 * q : 4 * q + 4, :].rearrange("a q c -> q a c"),
            )
        nc.sync.dma_start(tab_w[1][:], tab_words[1].rearrange("p t i -> p (t i)").bitcast(I32))
        nc.vector.tensor_copy(v_sc_rows[:], tab_sc[:].indirect(offs_sb[:]))
        for q in range(4):
            nc.sync.dma_start(
                v_sc[32 * q : 32 * q + 4].rearrange("p a c -> p (a c)").bitcast(I32),
                v_sc_rows[8 * q : 8 * q + 8, :].bitcast(I32),
            )

        w1_raw = {}
        z = {}

        def load_w1(b, a):
            w1_raw[b, a] = kept([PARTS, 4, PASS], F32, "w1_raw%d%d" % (b, a))
            rows = w1[PASS * a : PASS * (a + 1), PASS * b : PASS * (b + 1)]
            nc.sync.dma_start(w1_raw[b, a][:], rows.rearrange("(p j) c -> p j c", j=4))

        def load_patch(b, t):
            z[b, t] = kept([PARTS, S], F32, "z%d%d" % (b, t))
            rows = patch[PASS * b : PASS * (b + 1), :].rearrange("(p t) c -> t p c", t=4)
            nc.sync.dma_start(z[b, t][:], rows[t])

        load_w1(0, 0)
        load_w1(0, 1)
        load_patch(0, 0)
        nc.sync.dma_start(pos1_sb[:], pos1)
        load_patch(0, 1)
        load_patch(0, 2)
        load_w1(1, 0)
        load_patch(0, 3)
        load_w1(1, 1)
        for t in range(4):
            load_patch(1, t)
        res = []
        for i in range(4):
            res.append(kept([PARTS, P], F32, "res%d" % i))
            nc.sync.dma_start(res[i][:], matchup[PARTS * i : PARTS * (i + 1), :])

        nc.vector.tensor_copy(v_w[0][:], tab_w[0][:].bitcast(U32).indirect(offs_sb[:]))
        nc.vector.tensor_copy(
            w4_w[:].rearrange("p a c -> p (a c)").bitcast(U16).rearrange("p (n t m) -> p n t m", n=4, t=4),
            w4_raw[:].rearrange("p a c -> p (a c)").bitcast(U16).rearrange("p (n m t) -> p n t m", n=4, t=4),
        )
        nc.vector.tensor_copy(
            w4_sc[:].rearrange("p a (b t m) -> p (a b) t m", b=2, t=4),
            w4_sc_raw[:].rearrange("p a (b m t) -> p (a b) t m", b=2, t=4),
        )
        for half in range(2):
            nc.vector.tensor_copy(
                v_w[1][:, BANK * half : BANK * (half + 1)],
                tab_w[1][:].bitcast(U32).indirect(offs_sb[:, BANK // 16 * half : BANK // 16 * (half + 1)]),
            )

        nc.gpsimd.tensor_tensor(x2_mul[:], gain_sb[:, :, 0:4], trait_sb[:, :, 0:4], ALU.mult)
        nc.gpsimd.tensor_tensor(x2_add[:], side_sb[:, :, 0:4], trait_sb[:, :, 0:4], ALU.mult)

        w1_w = {}
        w1_sc = {}
        w1_bf = {}

        def round_w1(b, a, u, engine):
            if u == 0:
                w1_bf[b, a] = ring.tile([PARTS, 4, PASS], BF16, name="w1_bf", align_bytes=64)
                w1_w[b, a] = kept([PARTS, PASS], U32, "w1_w%d%d" % (b, a))
                w1_sc[b, a] = kept([PARTS, PASS], U8, "w1_sc%d%d" % (b, a))
            src = w1_raw[b, a][:].rearrange("p j (m t) -> p m j t", t=4)[:, :, :, 2 * u : 2 * u + 2]
            dst = w1_bf[b, a][:, 2 * u : 2 * u + 2, :].rearrange("p t (m j) -> p m j t", j=4)
            if engine == "vector":
                nc.vector.tensor_copy(dst, src)
            else:
                nc.scalar.copy(dst, src)

        def quantize_w1(b, a, t0, t1):
            cols = slice(PARTS * t0, PARTS * t1)
            nc.vector.quantize_mx(
                out=w1_w[b, a][:, cols].bitcast(FP8X4),
                scales=w1_sc[b, a][:, cols],
                in_=w1_bf[b, a][:, t0:t1, :].rearrange("p t c -> p (t c)"),
            )

        for a in range(2):
            round_w1(0, a, 0, "vector")
            round_w1(0, a, 1, "scalar")
            quantize_w1(0, a, 0, 1)
            quantize_w1(0, a, 1, 2)
            quantize_w1(0, a, 2, 4)

        def features(s):
            b, t = divmod(s, 4)
            for half in range(2):
                acc = bank((2 * s + half) % 4, "y_ps")
                cols = slice(BANK * half, BANK * (half + 1))
                for a in range(2):
                    c0 = PASS * b + PARTS * t
                    nc.tensor.matmul_mx(
                        out=acc[:],
                        lhsT=w4_w[:, a, 2 * c0 : 2 * (c0 + PARTS)].bitcast(FP4X4),
                        lhsT_scale=w4_sc[:, a, c0 : c0 + PARTS],
                        rhs=v_w[a][:, cols].bitcast(FP8X4),
                        rhs_scale=v_sc[:, a, cols],
                        start=(a == 0),
                        stop=False,
                    )
                for a in range(2):
                    nc.tensor.matmul_mx(
                        out=acc[:],
                        lhsT=w1_w[b, a][:, PARTS * t : PARTS * (t + 1)].bitcast(FP8X4),
                        lhsT_scale=w1_sc[b, a][:, PARTS * t : PARTS * (t + 1)],
                        rhs=v_w[a][:, cols].bitcast(FP8X4),
                        rhs_scale=v_sc[:, a, cols],
                        start=False,
                        stop=(a == 1),
                    )
                nc.vector.tensor_tensor(z[b, t][:, cols], acc[:], z[b, t][:, cols], ALU.add)
                nc.scalar.activation(z[b, t][:, cols], z[b, t][:, cols], ACT.Tanh)

        x1_rows = [kept([PARTS, 2, P, 2], BF16, "x1_rows%d" % b) for b in range(2)]
        x2_rows = [kept([PARTS, 2, P, 2], BF16, "x2_rows%d" % b) for b in range(2)]

        def pick2(s):
            b, t = divmod(s, 4)
            g2 = ring.tile([PARTS, P], F32, name="g2")
            nc.vector.tensor_copy(g2[:], z[b, t][:].indirect(pos2_sb[:]))
            nc.scalar.activation(x2_rows[b][:, t // 2, :, t % 2], g2[:], ACT.Identity, bias=x2_add[:, b, t : t + 1], scale=x2_mul[:, b, t : t + 1])

        def pick1(s, c0, c1):
            b, t = divmod(s, 4)
            g1 = ring.tile([PARTS, c1 - c0], F32, name="g1", bufs=4)
            nc.vector.tensor_copy(g1[:], z[b, t][:].indirect(pos1_sb[:, c0 // 16 : c1 // 16]))
            dst = x1_rows[b][:, t // 2, c0:c1, t % 2]
            if s < 6:
                nc.gpsimd.tensor_scalar(dst, g1[:], gain_sb[:, b, t : t + 1], 0.0, ALU.mult, ALU.add)
            else:
                nc.scalar.activation(dst, g1[:], ACT.Copy, scale=gain_sb[:, b, t : t + 1])

        x1_bf = [kept([PARTS, 4 * P], BF16, "x1_bf%d" % b) for b in range(2)]
        x2_bf = [kept([PARTS, 4 * P], BF16, "x2_bf%d" % b) for b in range(2)]
        x1_w = [kept([PARTS, P], U32, "x1_w%d" % b) for b in range(2)]
        x2_w = [kept([PARTS, P], U32, "x2_w%d" % b) for b in range(2)]
        x1_sc = [kept([PARTS, P], U8, "x1_sc%d" % b) for b in range(2)]
        x2_sc = [kept([PARTS, P], U8, "x2_sc%d" % b) for b in range(2)]

        def weave(dst, rows, c0, c1, engine):
            src = rows[:].rearrange("p u c e -> p u (c e)").bitcast(U32 if engine == "scalar" else I32)[:, :, c0:c1].rearrange("p u (c i) -> p c u i", i=4)
            dstv = dst[:].bitcast(U32 if engine == "scalar" else I32)[:, 2 * c0 : 2 * c1].rearrange("p (c i u) -> p c u i", i=4, u=2)
            if engine == "vector":
                nc.vector.tensor_copy(dstv, src)
            else:
                nc.scalar.copy(dstv, src)

        def quantize_x(words, scales, src, c0, c1):
            nc.vector.quantize_mx(out=words[:, c0:c1].bitcast(FP8X4), scales=scales[:, c0:c1], in_=src[:, 4 * c0 : 4 * c1])

        e_ps = {}

        def score(b, i):
            if b == 0:
                e_ps[i] = bank(4 + i, "e_ps")
            rows = slice(PARTS * i, PARTS * (i + 1))
            nc.tensor.matmul_mx(
                out=e_ps[i][:],
                lhsT=x1_w[b][:, rows].bitcast(FP8X4),
                lhsT_scale=x1_sc[b][:, rows],
                rhs=x2_w[b][:].bitcast(FP8X4),
                rhs_scale=x2_sc[b][:],
                start=(b == 0),
                stop=(b == 1),
            )

        for s in range(8):
            features(s)
            if s > 0:
                pick2(s - 1)
                pick1(s - 1, 0, P)
            if s in (1, 2):
                for u in range(2):
                    round_w1(1, s - 1, u, "scalar")
                quantize_w1(1, s - 1, 0, 4)
            if s == 4:
                weave(x2_bf[0], x2_rows[0], 0, P, "scalar")
                quantize_x(x2_w[0], x2_sc[0], x2_bf[0], 0, P)
            if s == 5:
                weave(x1_bf[0], x1_rows[0], 0, P, "scalar")
                quantize_x(x1_w[0], x1_sc[0], x1_bf[0], 0, P)
        for i in range(4):
            score(0, i)
        pick2(7)
        for i in range(4):
            pick1(7, PARTS * i, PARTS * (i + 1))
            weave(x1_bf[1], x1_rows[1], PARTS * i, PARTS * (i + 1), "scalar")
        weave(x2_bf[1], x2_rows[1], 0, P, "vector")
        quantize_x(x1_w[1], x1_sc[1], x1_bf[1], 0, PARTS)
        quantize_x(x2_w[1], x2_sc[1], x2_bf[1], 0, P)
        for i in range(4):
            if i > 0:
                quantize_x(x1_w[1], x1_sc[1], x1_bf[1], PARTS * i, PARTS * (i + 1))
            score(1, i)
        for i in range(4):
            for c0, c1 in ((0, P),) if i < 3 else ((0, P // 2), (P // 2, P)):
                nc.vector.tensor_tensor(res[i][:, c0:c1], e_ps[i][:, c0:c1], res[i][:, c0:c1], ALU.add)
                nc.scalar.activation(res[i][:, c0:c1], res[i][:, c0:c1], ACT.Sigmoid)
                nc.sync.dma_start(out[PARTS * i : PARTS * (i + 1), c0:c1], res[i][:, c0:c1])
